import numpy as np, ml_dtypes
CORES = [2,10,50,58,66,74,122]
N = 7
import mx_ref
BF = ml_dtypes.bfloat16
def entries(a):
    return np.ascontiguousarray(a.T).reshape(-1)
def table(e):
    return np.ascontiguousarray(np.reshape(e, (-1, 16)).T).astype(np.int32)
def cols(t, e):
    v = np.concatenate([t.reshape(128, -1, 4), np.zeros((128, 1, 4), BF)], axis=1)
    return np.ascontiguousarray(v[:, e]).reshape(128, -1)
def f(rng, *shape):
    return mx_ref.flush((rng.standard_normal(shape, dtype=np.float32) * np.exp2(rng.integers(-2, 3, shape[:-1] + (1,)))).astype(BF))
def wide(rng, *shape, cols=0):
    v = rng.standard_normal(shape, dtype=np.float32) * np.exp2(rng.integers(-12, 13, shape)).astype(np.float32)
    if cols: v *= np.repeat(np.exp2(rng.integers(-cols, cols + 1, shape[:-2] + (1, shape[-1] // 4))) * (rng.random(shape[:-2] + (1, shape[-1] // 4)) > 0.0625), 4, axis=-1).astype(np.float32)
    return mx_ref.flush(v.astype(BF))
T, NA, S, CAPP = 512, 512, 512, 96
def lists(rng, most=0, inorder=False, big=None):
    c, m = [], []
    for r in range(N):
        n = np.zeros(N, int)
        n[rng.permutation(N)[:most]] = CAPP
        while n.sum() < S:
            q = rng.integers(0, N)
            if n[q] < CAPP: n[q] += 1
        used = np.concatenate([q * CAPP + rng.permutation(CAPP)[:n[q]] for q in range(N)])
        slots = np.full(N * CAPP, -1); slots[used] = rng.integers(0, T, S)
        o = np.sort(used) if inorder else rng.permutation(used)
        if big is not None:
            for i in range(S // 32):
                k = o[32 * i + rng.integers(0, 32)]; slots[k] = rng.choice(big[k // CAPP])
        c.append(table(slots)); m.append(table(o))
    return {"want": np.stack(c), "slot": np.stack(m)}
def setup_inputs(rng):
    return {"v": f(rng, N, 128, 4 * T), "a": f(rng, N, 128, 4 * NA), **lists(rng)}
def setup_inputs_full(rng):
    return {**setup_inputs(rng), **lists(rng, most=S // CAPP)}
def setup_inputs_sorted(rng):
    return {**setup_inputs(rng), **lists(rng, inorder=True)}
def setup_inputs_giant(rng):
    d = setup_inputs(rng); big = [rng.permutation(T)[:T // 32] for q in range(N)]
    x = d["v"].reshape(N, 128, T, 4)
    for q in range(N): x[q][:, big[q]] = (x[q][:, big[q]].astype(np.float32) * np.float32(2.0 ** 20)).astype(BF)
    d["v"] = x.reshape(N, 128, 4 * T)
    return {**d, **lists(rng, big=big)}
def setup_inputs_spread(rng):
    d = setup_inputs(rng); d["v"] = wide(rng, N, 128, 4 * T); d["a"] = wide(rng, N, 128, 4 * NA); return d
def check_inputs(d):
    b = []
    for r in range(N):
        c, m = entries(d["want"][r]), entries(d["slot"][r])
        if c.min() < -1 or c.max() >= T or (c >= 0).sum() != S: b.append("want")
        if m.min() < 0 or m.max() >= N * CAPP or len(set(m.tolist())) != S or (c[np.clip(m, 0, N * CAPP - 1)] < 0).any(): b.append("slot")
    return b
def ones(b):
    e = np.zeros((128, 128, 4), np.float32); e[np.arange(128), np.arange(128), b] = 1
    return e.reshape(128, 512).astype(BF)
def decode(q):
    return np.stack([mx_ref.matmul(mx_ref.quantize(ones(b)), q) for b in range(4)], axis=1).reshape(512, -1)
def reference(v, a, want, slot, own=None):
    h = np.zeros((N, 128, 2048), BF); y = np.zeros((N, 128, 4 * NA), np.float32)
    for r in range(N):
        c = entries(want[r])
        arrived = np.concatenate([decode(mx_ref.quantize(cols(v[q], c[q * CAPP:(q + 1) * CAPP]))) for q in range(N)], axis=1)
        H = arrived[:, entries(slot[r])].T
        h[r] = H.reshape(128, 4, 512).transpose(0, 2, 1).reshape(128, 2048).astype(BF)
    for r in range(N):
        t = h[r] if own is None else np.asarray(own["h"][r])
        for o in range(4):
            y[r][:, NA * o:NA * o + NA] = mx_ref.matmul(mx_ref.quantize(np.ascontiguousarray(t[:, 512 * o:512 * o + 512])), mx_ref.quantize(a[r]))
    return {"y": y, "h": h}

@@ -1,0 +1,280 @@
+from concourse.bass import DstId, RemoteDMATransfer
+from concourse.mybir import dt, AluOpType, ActivationFunctionType
+
+CAPP = 96
+KO = CAPP // 16
+PAD = 32
+ASKS = ((1, 2), (3, 4, 5, 6))
+SERVES = ((1, 2), (3, 4), (5, 6))
+
+SCRATCH = {
+    "wants": ("sbuf", [128, 42], "int32"),
+    "slots": ("sbuf", [128, 32], "int32"),
+    "wraps": ("sbuf", [128, 32], "int32"),
+    "moved": ("sbuf", [128, 32], "int32"),
+    "ask": ("sbuf", [128, 42], "uint16"),
+    "asked": ("sbuf", [128, 36], "uint16"),
+    "place": ("sbuf", [128, 32], "uint16"),
+    "vt": ("sbuf", [128, 2048], "bfloat16"),
+    "at": ("sbuf", [128, 2048], "bfloat16"),
+    "pickO": ("sbuf", [128, 512], "bfloat16"),
+    "gotc": ("sbuf", [128, PAD + 7 * CAPP], "float8_e4m3fn_x4"),
+    "gots": ("sbuf", [128, PAD + 7 * CAPP], "uint8"),
+    "num": ("sbuf", [128, 512], "bfloat16"),
+    "row": ("sbuf", [128, 4], "float32"),
+    "eye": ("sbuf", [128, 2048], "bfloat16"),
+    "eyec": ("sbuf", [128, 512], "float8_e4m3fn_x4"),
+    "eyes": ("sbuf", [128, 512], "uint8"),
+    "ones": ("sbuf", [128, 128], "float32"),
+    "ident": ("sbuf", [128, 128], "float32"),
+    "ht": ("sbuf", [128, 2048], "bfloat16"),
+    "hc": ("sbuf", [128, 512], "float8_e4m3fn_x4"),
+    "hs": ("sbuf", [128, 512], "uint8"),
+    "ac": ("sbuf", [128, 512], "float8_e4m3fn_x4"),
+    "ascale": ("sbuf", [128, 512], "uint8"),
+    "yt": ("sbuf", [128, 2048], "float32"),
+}
+for _x in range(3):
+    SCRATCH["pick%d" % _x] = ("sbuf", [128, 8 * CAPP], "bfloat16")
+    SCRATCH["code%d" % _x] = ("sbuf", [128, 2 * CAPP], "float8_e4m3fn_x4")
+    SCRATCH["scal%d" % _x] = ("sbuf", [128, 2 * CAPP], "uint8")
+for _o in range(4):
+    SCRATCH["win%d" % _o] = ("sbuf", [128, 7 * CAPP], "bfloat16")
+    SCRATCH["ord%d" % _o] = ("sbuf", [128, 512], "float32")
+for _b in range(8):
+    SCRATCH["bank%d" % _b] = ("psum", [128, 512], "float32")
+
+SEMAPHORES = ["want", "vin", "slotin", "ain", "asks", "consts", "one", "pad", "id", "eyeb", "eyeq", "lsent",
+              "list0", "list1", "gO", "qO", "p1", "p2", "p3", "qa", "dsent",
+              "my0", "my1", "my2", "my3a", "my3b", "yc0", "yc1", "yc2", "yc3a", "yc3b", "out"]
+for _x in range(3):
+    SEMAPHORES += ["gat%d" % _x, "qua%d" % _x, "data%d" % _x]
+for _o in range(4):
+    SEMAPHORES += ["ua%d" % _o, "ub%d" % _o, "uc%d" % _o, "x%d" % _o, "w%d" % _o, "g%d" % _o, "t%d" % _o, "tl%d" % _o,
+                   "hc%d" % _o, "qh%d" % _o]
+
+
+def fused(g, core, topo, parts, remote_sem, local_sem):
+    engines = [e for e in topo.engines(core, parts[0][0]) if all(e in topo.engines(core, d) for d, _, _ in parts)]
+    w = 1
+    while 2 * w * len(parts) <= len(engines):
+        w *= 2
+    transfers = []
+    for i, (d, src, dst) in enumerate(parts):
+        rid, pid, _ = topo.addr(d)
+        transfers.append(RemoteDMATransfer(dst_ids=[DstId(rid=rid, pnc=pid)],
+                                           dma_engine_mask=sum(1 << e for e in engines[i * w:(i + 1) * w]),
+                                           remote_sem=remote_sem, src=src, dst=dst))
+    g.remote_dma_fused(transfers, local_sem=local_sem)
+    return w
+
+
+def rank_program(g, core, T, topo):
+    rank = T.rank_of(core)
+    if rank is None:
+        return
+    N = len(T.cores)
+    S = T.sem
+    V, A, P, D = g.vector, g.scalar, g.tensor, g.sync
+    Copy = ActivationFunctionType.Copy
+    bank = [T["bank%d" % b] for b in range(8)]
+    win = [T["win%d" % o] for o in range(4)]
+    ordd = [T["ord%d" % o] for o in range(4)]
+
+    for k in range(4):
+        D.dma_start(T.wants[16 * k:16 * k + 16, :], T.want[:]).then_inc(S.want, 16)
+        A.dma_start(T.wants[64 + 16 * k:64 + 16 * k + 16, :], T.want[:]).then_inc(S.want, 16)
+    D.dma_start(T.vt[:], T.v[:]).then_inc(S.vin, 16)
+
+    g.iota(T.row[:], [[1, 4]], -256, 4, allow_small_or_imprecise_dtypes=True).then_inc(S.consts, 1)
+    g.iota(T.num[:], [[1, 512]], -256, 0, allow_small_or_imprecise_dtypes=True).then_inc(S.consts, 1)
+    g.wait_ge(S.asks, 1)
+    listed = []
+    for x, ds in enumerate(ASKS):
+        parts = []
+        for d in ds:
+            q = (rank + d) % N
+            parts.append((T.cores[q], T.ask[:, KO * q:KO * q + KO], T.asked[:, KO * (d - 1):KO * d]))
+        listed.append(len(parts) * fused(g, core, topo, parts, S["list%d" % x], S.lsent))
+    g.wait_ge(S.one, 1)
+    g.affine_select(T.ident[:], T.ones[:], [[-1, 128]], AluOpType.is_equal, 0.0, 0, 1).then_inc(S.id, 1)
+
+    D.wait_ge(S.lsent, sum(listed))
+    D.dma_start(T.at[:], T.a[:]).then_inc(S.ain, 16)
+    for k in range(8):
+        D.dma_start(T.slots[16 * k:16 * k + 16, :], T.slot[:]).then_inc(S.slotin, 16)
+
+    V.memset(T.ones[:], 1.0).then_inc(S.one, 1)
+    V.memset(T.pickO[:, 0:4 * PAD], 0.0).then_inc(S.pad, 1)
+    V.wait_ge(S.want, 128)
+    V.tensor_scalar(T.ask[:], T.wants[:], 4.0, 0.0, AluOpType.mult, AluOpType.max).then_inc(S.asks, 1)
+    V.wait_ge(S.consts, 2)
+    for t in range(4):
+        V.tensor_scalar(T.eye[:, t:2048:4], T.num[:], T.row[:, t:t + 1], None, AluOpType.is_equal).then_inc(S.eyeb, 1)
+    V.wait_ge(S.eyeb, 4)
+    V.quantize_mx(T.eyec[:], T.eyes[:], T.eye[:]).then_inc(S.eyeq, 1)
+
+    def pick(tile, lo, offsets, sem):
+        n4 = tile.shape[1]
+        for t in (0, 1):
+            V.tensor_copy(tile[:, lo + t:n4:4], T.vt[:, t:2048].indirect(offsets)).then_inc(sem, 1)
+        for t in (2, 3):
+            A.activation(tile[:, lo + t:n4:4], T.vt[:, t:2048].indirect(offsets), Copy).then_inc(sem, 1)
+
+    V.wait_ge(S.vin, 16)
+    A.wait_ge(S.vin, 16)
+    sent = []
+    for x, ds in enumerate(SERVES):
+        if x < 2:
+            V.wait_ge(S["list%d" % x], listed[x])
+            A.wait_ge(S["list%d" % x], listed[x])
+        gs, qs = S["gat%d" % x], S["qua%d" % x]
+        code, scal, tile = T["code%d" % x], T["scal%d" % x], T["pick%d" % x]
+        pick(tile, 0, T.asked[:, KO * (ds[0] - 1):KO * ds[-1]], gs)
+        V.wait_ge(gs, 4)
+        V.quantize_mx(code[:], scal[:], tile[:]).then_inc(qs, 1)
+        g.wait_ge(qs, 1)
+        cparts, sparts = [], []
+        for i, d in enumerate(ds):
+            dst = T.cores[(rank - d) % N]
+            to = PAD + CAPP * d
+            cparts.append((dst, code[:, CAPP * i:CAPP * i + CAPP].bitcast(dt.uint8), T.gotc[:, to:to + CAPP].bitcast(dt.uint8)))
+            sparts.append((dst, scal[:, CAPP * i:CAPP * i + CAPP], T.gots[:, to:to + CAPP]))
+        sent.append(0)
+        for parts in (cparts, sparts):
+            sent[-1] += len(parts) * fused(g, core, topo, parts, S["data%d" % x], S.dsent)
+
+    V.wait_ge(S.asks, 1)
+    A.wait_ge(S.asks, 1)
+    pick(T.pickO, 4 * PAD, T.ask[:, KO * rank:KO * rank + KO], S.gO)
+    V.wait_ge(S.gO, 4)
+    V.wait_ge(S.pad, 1)
+    V.quantize_mx(T.gotc[:, 0:PAD + CAPP], T.gots[:, 0:PAD + CAPP], T.pickO[:]).then_inc(S.qO, 1)
+    V.wait_ge(S.slotin, 128)
+    V.tensor_scalar(T.wraps[:], T.slots[:], float(CAPP * rank), float(CAPP * N), AluOpType.is_lt, AluOpType.mult).then_inc(S.p1, 1)
+    V.wait_ge(S.p1, 1)
+    V.tensor_tensor(T.moved[:], T.slots[:], T.wraps[:], AluOpType.add).then_inc(S.p2, 1)
+    V.wait_ge(S.p2, 1)
+    V.tensor_scalar(T.place[:], T.moved[:], float(CAPP * rank), None, AluOpType.subtract).then_inc(S.p3, 1)
+    V.wait_ge(S.ain, 16)
+    V.quantize_mx(T.ac[:], T.ascale[:], T.at[:]).then_inc(S.qa, 1)
+
+    spans = ((0, 3 * CAPP, 0, "ua%d"), (3 * CAPP, 2 * CAPP, 4, "ub%d"), (5 * CAPP, 2 * CAPP, 0, "uc%d"))
+    P.wait_ge(S.eyeq, 1)
+    P.wait_ge(S.qO, 1)
+    for x, (lo, n, b, u) in enumerate(spans):
+        P.wait_ge(S["data%d" % x], sent[x])
+        for o in range(4):
+            if x == 2:
+                P.wait_ge(S["x%d" % o], 1)
+            P.matmul_mx(bank[b + o][:, 0:n], T.eyec[:, 128 * o:128 * o + 128], T.eyes[:, 128 * o:128 * o + 128],
+                        T.gotc[:, PAD + lo:PAD + lo + n], T.gots[:, PAD + lo:PAD + lo + n], True, True).then_inc(S[u % o], 1)
+
+    def window(x, o):
+        lo, n, b, u = spans[x]
+        out, src, sem = win[o][:, lo:lo + n], bank[b + o][:, 0:n], S[("w%d" if x else "x%d") % o]
+        if o % 2:
+            A.wait_ge(S[u % o], 1)
+            A.activation(out, src, Copy).then_inc(sem, 1)
+        else:
+            V.wait_ge(S[u % o], 1)
+            V.tensor_copy(out, src).then_inc(sem, 1)
+
+    def order(o):
+        V.wait_ge(S["w%d" % o], 2)
+        V.tensor_copy(ordd[o][:, 0:256], win[o][:].indirect(T.place[:, 0:16])).then_inc(S["g%d" % o], 1)
+        A.wait_ge(S["w%d" % o], 2)
+        A.activation(ordd[o][:, 256:512], win[o][:].indirect(T.place[:, 16:32]), Copy).then_inc(S["g%d" % o], 1)
+
+    for x in (0, 1):
+        for o in range(4):
+            window(x, o)
+    V.wait_ge(S.p3, 1)
+    A.wait_ge(S.p3, 1)
+    window(2, 0)
+    window(2, 1)
+    order(0)
+    window(2, 2)
+    window(2, 3)
+    order(1)
+    order(2)
+    order(3)
+
+    last = (7, 3, 4, 5)
+
+    def turn(o):
+        P.wait_ge(S["g%d" % o], 2)
+        for t in range(4):
+            out, sem = (bank[4 + o][:, t:512:4], S["t%d" % o]) if o < 3 else (bank[last[t]][:, 0:128], S["tl%d" % t])
+            P.transpose(out, ordd[o][:, t:512:4], T.ident[:]).then_inc(sem, 1)
+
+    def product(o, out, lo, n, sem):
+        P.matmul_mx(out, T.hc[:, 128 * o:128 * o + 128], T.hs[:, 128 * o:128 * o + 128],
+                    T.ac[:, lo:lo + n], T.ascale[:, lo:lo + n], True, True).then_inc(sem, 1)
+
+    P.wait_ge(S.id, 1)
+    turn(0)
+    turn(1)
+    P.wait_ge(S.qa, 1)
+    for o in range(4):
+        P.wait_ge(S["qh%d" % o], 1)
+        if o < 3:
+            product(o, bank[o][:], 0, 512, S["my%d" % o])
+        else:
+            product(o, bank[6][:, 0:256], 0, 256, S.my3a)
+            product(o, bank[7][:, 0:256], 256, 256, S.my3b)
+        if o < 2:
+            turn(o + 2)
+
+    def out_of(q, out, src, wait, n, sem):
+        q.wait_ge(wait, n)
+        if q is V:
+            V.tensor_copy(out, src).then_inc(sem, 1)
+        else:
+            A.activation(out, src, Copy).then_inc(sem, 1)
+
+    def hcopy(q, o):
+        out_of(q, T.ht[:, 512 * o:512 * o + 512], bank[4 + o][:], S["t%d" % o], 4, S["hc%d" % o])
+
+    def hlast(q, t):
+        out_of(q, T.ht[:, 1536 + t:2048:4], bank[last[t]][:, 0:128], S["tl%d" % t], 1, S.hc3)
+
+    def hquant(o):
+        V.wait_ge(S["hc%d" % o], 1 if o < 3 else 4)
+        V.quantize_mx(T.hc[:, 128 * o:128 * o + 128], T.hs[:, 128 * o:128 * o + 128],
+                      T.ht[:, 512 * o:512 * o + 512]).then_inc(S["qh%d" % o], 1)
+
+    def ycopy(q, o):
+        out_of(q, T.yt[:, 512 * o:512 * o + 512], bank[o][:], S["my%d" % o], 1, S["yc%d" % o])
+
+    hquant(0)
+    hcopy(V, 1)
+    hquant(1)
+    ycopy(V, 1)
+    hquant(2)
+    hlast(V, 0)
+    hlast(V, 2)
+    hquant(3)
+    out_of(V, T.yt[:, 1536:1792], bank[6][:, 0:256], S.my3a, 1, S.yc3a)
+
+    hcopy(A, 0)
+    ycopy(A, 0)
+    hcopy(A, 2)
+    hlast(A, 1)
+    hlast(A, 3)
+    ycopy(A, 2)
+    out_of(A, T.yt[:, 1792:2048], bank[7][:, 0:256], S.my3b, 1, S.yc3b)
+    A.wait_ge(S.yc3b, 1)
+    A.dma_start(T.y[:, 1792:2048], T.yt[:, 1792:2048]).then_inc(S.out, 16)
+
+    for kind, o in (("h", 0), ("h", 1), ("y", 0), ("h", 2), ("y", 1), ("h", 3), ("y", 2)):
+        if kind == "h":
+            D.wait_ge(S["hc%d" % o], 1 if o < 3 else 4)
+            D.dma_start(T.h[:, 512 * o:512 * o + 512], T.ht[:, 512 * o:512 * o + 512]).then_inc(S.out, 16)
+        else:
+            D.wait_ge(S["yc%d" % o], 1)
+            D.dma_start(T.y[:, 512 * o:512 * o + 512], T.yt[:, 512 * o:512 * o + 512]).then_inc(S.out, 16)
+    D.wait_ge(S.yc3a, 1)
+    D.dma_start(T.y[:, 1536:1792], T.yt[:, 1536:1792]).then_inc(S.out, 16)
+    D.wait_ge(S.out, 16 * 9)
+    g.wait_ge(S.dsent, sum(sent))

@@ -4,28 +4,35 @@ from concourse.mybir import dt, AluOpType, ActivationFunctionType
 CAPP = 96
 KO = CAPP // 16
 PAD = 32
+WIN = 7 * CAPP
 ASKS = ((1, 2), (3, 4, 5, 6))
 SERVES = ((1, 2), (3, 4), (5, 6))
 
+TENSOR = ("unpack0 unpack3 unpack1 unpack2 turn00 turn01 turn02 turn03 turn10 turn11 turn12 turn13 product0 "
+          "turn20 turn21 turn22 turn23 product1 product20 product21 product3")
+VECTOR = "window0 half0 order3 fold3 hcopy0 quant0 hcopy1 hcopy20 quant1 hcopy22 hcopy23 quant2 quant3 ycopy21"
+SCALAR = "window3 half0 window1 order1 window2 order2 ycopy0 hcopy21 ycopy1 ycopy20 ycopy3"
+SYNC = "spread3 hstore0 hstore1 ystore0 hstore2 hstore3 ystore1 ystore2 ystore3"
+
 SCRATCH = {
     "wants": ("sbuf", [128, 42], "int32"),
-    "slots": ("sbuf", [128, 32], "int32"),
-    "wraps": ("sbuf", [128, 32], "int32"),
-    "moved": ("sbuf", [128, 32], "int32"),
+    "slots": ("sbuf", [128, 48], "int32"),
+    "wraps": ("sbuf", [128, 48], "int32"),
+    "moved": ("sbuf", [128, 64], "float32"),
+    "movt": ("sbuf", [128, 32], "float32"),
     "ask": ("sbuf", [128, 42], "uint16"),
     "asked": ("sbuf", [128, 36], "uint16"),
     "place": ("sbuf", [128, 32], "uint16"),
+    "placq": ("sbuf", [128, 32], "uint16"),
     "vt": ("sbuf", [128, 2048], "bfloat16"),
     "at": ("sbuf", [128, 2048], "bfloat16"),
     "pickO": ("sbuf", [128, 512], "bfloat16"),
-    "gotc": ("sbuf", [128, PAD + 7 * CAPP], "float8_e4m3fn_x4"),
-    "gots": ("sbuf", [128, PAD + 7 * CAPP], "uint8"),
+    "gotc": ("sbuf", [128, PAD + WIN], "float8_e4m3fn_x4"),
+    "gots": ("sbuf", [128, PAD + WIN], "uint8"),
     "num": ("sbuf", [128, 512], "bfloat16"),
-    "row": ("sbuf", [128, 4], "float32"),
     "eye": ("sbuf", [128, 2048], "bfloat16"),
     "eyec": ("sbuf", [128, 512], "float8_e4m3fn_x4"),
     "eyes": ("sbuf", [128, 512], "uint8"),
-    "ones": ("sbuf", [128, 128], "float32"),
     "ident": ("sbuf", [128, 128], "float32"),
     "ht": ("sbuf", [128, 2048], "bfloat16"),
     "hc": ("sbuf", [128, 512], "float8_e4m3fn_x4"),
@@ -39,19 +46,22 @@ for _x in range(3):
     SCRATCH["code%d" % _x] = ("sbuf", [128, 2 * CAPP], "float8_e4m3fn_x4")
     SCRATCH["scal%d" % _x] = ("sbuf", [128, 2 * CAPP], "uint8")
 for _o in range(4):
-    SCRATCH["win%d" % _o] = ("sbuf", [128, 7 * CAPP], "bfloat16")
-    SCRATCH["ord%d" % _o] = ("sbuf", [128, 512], "float32")
+    SCRATCH["win%d" % _o] = ("sbuf", [128, WIN], "bfloat16")
+    if "fold%d" % _o in VECTOR:
+        SCRATCH["ordq%d" % _o] = ("sbuf", [128, 512], "bfloat16")
+        SCRATCH["turned%d" % _o] = ("sbuf", [128, 512], "bfloat16")
+    else:
+        SCRATCH["ord%d" % _o] = ("sbuf", [128, 512], "float32")
 for _b in range(8):
     SCRATCH["bank%d" % _b] = ("psum", [128, 512], "float32")
 
-SEMAPHORES = ["want", "vin", "slotin", "ain", "asks", "consts", "one", "pad", "id", "eyeb", "eyeq", "lsent",
-              "list0", "list1", "gO", "qO", "p1", "p2", "p3", "qa", "dsent",
-              "my0", "my1", "my2", "my3a", "my3b", "yc0", "yc1", "yc2", "yc3a", "yc3b", "out"]
+SEMAPHORES = ["want", "vin", "slotin", "ain", "asks", "consts", "pad", "id", "eyeb", "eyeq", "lsent",
+              "list0", "list1", "gO", "qO", "p1", "p2", "p3", "q2", "q3", "qa", "dsent", "early0", "early1", "out"]
 for _x in range(3):
     SEMAPHORES += ["gat%d" % _x, "qua%d" % _x, "data%d" % _x]
 for _o in range(4):
-    SEMAPHORES += ["ua%d" % _o, "ub%d" % _o, "uc%d" % _o, "x%d" % _o, "w%d" % _o, "g%d" % _o, "t%d" % _o, "tl%d" % _o,
-                   "hc%d" % _o, "qh%d" % _o]
+    SEMAPHORES += [_c + "%d" % _o for _c in ("w", "g", "vt", "h", "qh", "y")]
+    SEMAPHORES += ["u%d%d" % (_x, _o) for _x in range(3)] + ["t%d%d" % (_o, _x) for _x in range(4)] + ["m%d0" % _o, "m%d1" % _o]
 
 
 def fused(g, core, topo, parts, remote_sem, local_sem):
@@ -79,15 +89,28 @@ def rank_program(g, core, T, topo):
     Copy = ActivationFunctionType.Copy
     bank = [T["bank%d" % b] for b in range(8)]
     win = [T["win%d" % o] for o in range(4)]
-    ordd = [T["ord%d" % o] for o in range(4)]
+
+    def move(q, out, src, sem):
+        if q is V:
+            V.tensor_copy(out, src).then_inc(sem, 1)
+        else:
+            A.activation(out, src, Copy).then_inc(sem, 1)
+
+    def out_of(q, out, src, wait, n, sem):
+        q.wait_ge(wait, n)
+        move(q, out, src, sem)
 
     for k in range(4):
         D.dma_start(T.wants[16 * k:16 * k + 16, :], T.want[:]).then_inc(S.want, 16)
         A.dma_start(T.wants[64 + 16 * k:64 + 16 * k + 16, :], T.want[:]).then_inc(S.want, 16)
     D.dma_start(T.vt[:], T.v[:]).then_inc(S.vin, 16)
+    for k in range(2):
+        D.dma_start(T.slots[16 * k:16 * k + 16, 0:32], T.slot[:]).then_inc(S.slotin, 16)
+    for t in range(4):
+        D.dma_start(T.slots[8 * t:8 * t + 8, 32:48], T.slot[t:16:4, :]).then_inc(S.slotin, 16)
+    D.dma_start(T.at[:], T.a[:]).then_inc(S.ain, 16)
 
-    g.iota(T.row[:], [[1, 4]], -256, 4, allow_small_or_imprecise_dtypes=True).then_inc(S.consts, 1)
-    g.iota(T.num[:], [[1, 512]], -256, 0, allow_small_or_imprecise_dtypes=True).then_inc(S.consts, 1)
+    g.iota(T.num[:], [[1, 512]], 0, -4, allow_small_or_imprecise_dtypes=True).then_inc(S.consts, 1)
     g.wait_ge(S.asks, 1)
     listed = []
     for x, ds in enumerate(ASKS):
@@ -96,41 +119,34 @@ def rank_program(g, core, T, topo):
             q = (rank + d) % N
             parts.append((T.cores[q], T.ask[:, KO * q:KO * q + KO], T.asked[:, KO * (d - 1):KO * d]))
         listed.append(len(parts) * fused(g, core, topo, parts, S["list%d" % x], S.lsent))
-    g.wait_ge(S.one, 1)
-    g.affine_select(T.ident[:], T.ones[:], [[-1, 128]], AluOpType.is_equal, 0.0, 0, 1).then_inc(S.id, 1)
 
-    D.wait_ge(S.lsent, sum(listed))
-    D.dma_start(T.at[:], T.a[:]).then_inc(S.ain, 16)
-    for k in range(8):
-        D.dma_start(T.slots[16 * k:16 * k + 16, :], T.slot[:]).then_inc(S.slotin, 16)
-
-    V.memset(T.ones[:], 1.0).then_inc(S.one, 1)
     V.memset(T.pickO[:, 0:4 * PAD], 0.0).then_inc(S.pad, 1)
     V.wait_ge(S.want, 128)
     V.tensor_scalar(T.ask[:], T.wants[:], 4.0, 0.0, AluOpType.mult, AluOpType.max).then_inc(S.asks, 1)
-    V.wait_ge(S.consts, 2)
+    V.wait_ge(S.consts, 1)
     for t in range(4):
-        V.tensor_scalar(T.eye[:, t:2048:4], T.num[:], T.row[:, t:t + 1], None, AluOpType.is_equal).then_inc(S.eyeb, 1)
+        V.tensor_scalar(T.eye[:, t:2048:4], T.num[:], float(t), None, AluOpType.is_equal).then_inc(S.eyeb, 1)
+    V.tensor_scalar(T.ident[:], T.num[:, 0:512:4], 0.0, None, AluOpType.is_equal).then_inc(S.id, 1)
     V.wait_ge(S.eyeb, 4)
     V.quantize_mx(T.eyec[:], T.eyes[:], T.eye[:]).then_inc(S.eyeq, 1)
 
-    def pick(tile, lo, offsets, sem):
+    def pick(tile, lo, offsets, sem, who):
         n4 = tile.shape[1]
-        for t in (0, 1):
-            V.tensor_copy(tile[:, lo + t:n4:4], T.vt[:, t:2048].indirect(offsets)).then_inc(sem, 1)
-        for t in (2, 3):
-            A.activation(tile[:, lo + t:n4:4], T.vt[:, t:2048].indirect(offsets), Copy).then_inc(sem, 1)
+        for t in range(4):
+            move(who[t], tile[:, lo + t:n4:4], T.vt[:, t:2048].indirect(offsets), sem)
 
     V.wait_ge(S.vin, 16)
     A.wait_ge(S.vin, 16)
-    sent = []
+    A.wait_ge(S.asks, 1)
+    pick(T.pickO, 4 * PAD, T.ask[:, KO * rank:KO * rank + KO], S.gO, (A, A, A, A))
+    sent = [0, 0, 0]
     for x, ds in enumerate(SERVES):
-        if x < 2:
+        if x < len(ASKS):
             V.wait_ge(S["list%d" % x], listed[x])
             A.wait_ge(S["list%d" % x], listed[x])
         gs, qs = S["gat%d" % x], S["qua%d" % x]
         code, scal, tile = T["code%d" % x], T["scal%d" % x], T["pick%d" % x]
-        pick(tile, 0, T.asked[:, KO * (ds[0] - 1):KO * ds[-1]], gs)
+        pick(tile, 0, T.asked[:, KO * (ds[0] - 1):KO * ds[-1]], gs, (V, V, A, A))
         V.wait_ge(gs, 4)
         V.quantize_mx(code[:], scal[:], tile[:]).then_inc(qs, 1)
         g.wait_ge(qs, 1)
@@ -140,141 +156,151 @@ def rank_program(g, core, T, topo):
             to = PAD + CAPP * d
             cparts.append((dst, code[:, CAPP * i:CAPP * i + CAPP].bitcast(dt.uint8), T.gotc[:, to:to + CAPP].bitcast(dt.uint8)))
             sparts.append((dst, scal[:, CAPP * i:CAPP * i + CAPP], T.gots[:, to:to + CAPP]))
-        sent.append(0)
         for parts in (cparts, sparts):
-            sent[-1] += len(parts) * fused(g, core, topo, parts, S["data%d" % x], S.dsent)
+            sent[x] += len(parts) * fused(g, core, topo, parts, S["data%d" % x], S.dsent)
 
-    V.wait_ge(S.asks, 1)
-    A.wait_ge(S.asks, 1)
-    pick(T.pickO, 4 * PAD, T.ask[:, KO * rank:KO * rank + KO], S.gO)
     V.wait_ge(S.gO, 4)
     V.wait_ge(S.pad, 1)
     V.quantize_mx(T.gotc[:, 0:PAD + CAPP], T.gots[:, 0:PAD + CAPP], T.pickO[:]).then_inc(S.qO, 1)
-    V.wait_ge(S.slotin, 128)
-    V.tensor_scalar(T.wraps[:], T.slots[:], float(CAPP * rank), float(CAPP * N), AluOpType.is_lt, AluOpType.mult).then_inc(S.p1, 1)
+    first, add, sub = float(CAPP * rank), AluOpType.add, AluOpType.subtract
+    V.wait_ge(S.slotin, 96)
+    V.tensor_scalar(T.wraps[0:32, :], T.slots[0:32, :], first, float(WIN), AluOpType.is_lt, AluOpType.mult).then_inc(S.p1, 1)
     V.wait_ge(S.p1, 1)
-    V.tensor_tensor(T.moved[:], T.slots[:], T.wraps[:], AluOpType.add).then_inc(S.p2, 1)
-    V.wait_ge(S.p2, 1)
-    V.tensor_scalar(T.place[:], T.moved[:], float(CAPP * rank), None, AluOpType.subtract).then_inc(S.p3, 1)
+    V.tensor_tensor(T.moved[0:32, 0:48], T.slots[0:32, :], T.wraps[0:32, :], add).then_inc(S.q2, 1)
+    V.tensor_tensor(T.moved[0:32, 48:64], T.slots[0:32, 32:48], T.wraps[0:32, 32:48], add).then_inc(S.q2, 1)
+    A.wait_ge(S.q2, 2)
+    for k in range(1, 4):
+        move(A, T.moved[32 * k:32 * k + 32, :], T.moved[0:32, :], S.p2)
     V.wait_ge(S.ain, 16)
     V.quantize_mx(T.ac[:], T.ascale[:], T.at[:]).then_inc(S.qa, 1)
+    V.wait_ge(S.q2, 2)
+    V.wait_ge(S.p2, 3)
+    V.transpose(T.movt[:], T.moved[:, 32:64]).then_inc(S.q3, 1)
+    V.tensor_scalar(T.place[:], T.moved[:, 0:32], first, None, sub).then_inc(S.p3, 1)
+    V.wait_ge(S.q3, 1)
+    V.tensor_scalar(T.placq[:], T.movt[:], first, None, sub).then_inc(S.p3, 1)
 
-    spans = ((0, 3 * CAPP, 0, "ua%d"), (3 * CAPP, 2 * CAPP, 4, "ub%d"), (5 * CAPP, 2 * CAPP, 0, "uc%d"))
+    spans = ((0, 3 * CAPP, 0), (3 * CAPP, 2 * CAPP, 4), (5 * CAPP, 2 * CAPP, 0))
+
+    def unpack(o, x=2):
+        lo, n, b = spans[x]
+        P.matmul_mx(bank[b + o][:, 0:n], T.eyec[:, 128 * o:128 * o + 128], T.eyes[:, 128 * o:128 * o + 128],
+                    T.gotc[:, PAD + lo:PAD + lo + n], T.gots[:, PAD + lo:PAD + lo + n], True, True).then_inc(S["u%d%d" % (x, o)], 1)
+
+    def window(q, o, x=2):
+        lo, n, b = spans[x]
+        out_of(q, win[o][:, lo:lo + n], bank[b + o][:, 0:n], S["u%d%d" % (x, o)], 1, S["w%d" % o if x == 2 else "early%d" % x])
+
     P.wait_ge(S.eyeq, 1)
-    P.wait_ge(S.qO, 1)
-    for x, (lo, n, b, u) in enumerate(spans):
-        P.wait_ge(S["data%d" % x], sent[x])
-        for o in range(4):
-            if x == 2:
-                P.wait_ge(S["x%d" % o], 1)
-            P.matmul_mx(bank[b + o][:, 0:n], T.eyec[:, 128 * o:128 * o + 128], T.eyes[:, 128 * o:128 * o + 128],
-                        T.gotc[:, PAD + lo:PAD + lo + n], T.gots[:, PAD + lo:PAD + lo + n], True, True).then_inc(S[u % o], 1)
-
-    def window(x, o):
-        lo, n, b, u = spans[x]
-        out, src, sem = win[o][:, lo:lo + n], bank[b + o][:, 0:n], S[("w%d" if x else "x%d") % o]
-        if o % 2:
-            A.wait_ge(S[u % o], 1)
-            A.activation(out, src, Copy).then_inc(sem, 1)
-        else:
-            V.wait_ge(S[u % o], 1)
-            V.tensor_copy(out, src).then_inc(sem, 1)
-
-    def order(o):
-        V.wait_ge(S["w%d" % o], 2)
-        V.tensor_copy(ordd[o][:, 0:256], win[o][:].indirect(T.place[:, 0:16])).then_inc(S["g%d" % o], 1)
-        A.wait_ge(S["w%d" % o], 2)
-        A.activation(ordd[o][:, 256:512], win[o][:].indirect(T.place[:, 16:32]), Copy).then_inc(S["g%d" % o], 1)
-
-    for x in (0, 1):
-        for o in range(4):
-            window(x, o)
-    V.wait_ge(S.p3, 1)
-    A.wait_ge(S.p3, 1)
-    window(2, 0)
-    window(2, 1)
-    order(0)
-    window(2, 2)
-    window(2, 3)
-    order(1)
-    order(2)
-    order(3)
-
-    last = (7, 3, 4, 5)
-
-    def turn(o):
-        P.wait_ge(S["g%d" % o], 2)
-        for t in range(4):
-            out, sem = (bank[4 + o][:, t:512:4], S["t%d" % o]) if o < 3 else (bank[last[t]][:, 0:128], S["tl%d" % t])
-            P.transpose(out, ordd[o][:, t:512:4], T.ident[:]).then_inc(sem, 1)
-
-    def product(o, out, lo, n, sem):
-        P.matmul_mx(out, T.hc[:, 128 * o:128 * o + 128], T.hs[:, 128 * o:128 * o + 128],
-                    T.ac[:, lo:lo + n], T.ascale[:, lo:lo + n], True, True).then_inc(sem, 1)
-
     P.wait_ge(S.id, 1)
-    turn(0)
-    turn(1)
+    P.wait_ge(S.qO, 1)
+    for x in (0, 1):
+        P.wait_ge(S["data%d" % x], sent[x])
+        for o in (0, 3, 1, 2):
+            unpack(o, x)
+            window(A if o < 2 else V, o, x)
+        for q in (V, A):
+            if x == 0:
+                q.wait_ge(S.p3, 2)
+            q.wait_ge(S["early%d" % x], 4)
     P.wait_ge(S.qa, 1)
-    for o in range(4):
-        P.wait_ge(S["qh%d" % o], 1)
-        if o < 3:
-            product(o, bank[o][:], 0, 512, S["my%d" % o])
+    P.wait_ge(S.early0, 4)
+    P.wait_ge(S.data2, sent[2])
+
+    names = (TENSOR + " " + VECTOR + " " + SCALAR).split()
+    folded = [o for o in range(4) if "fold%d" % o in names]
+    gathered = [(S["g%d" % o], 2 if "half%d" % o in names else 1) for o in range(4)]
+    hready = [(S["h%d" % o], 64 if o in folded else 1 if "hcopy%d" % o in names else 4) for o in range(4)]
+    yready = [(S["y%d" % o], 1 if "ycopy%d" % o in names else 2) for o in range(4)]
+    freed = [(S["w%d" % b], 1) for b in range(4)] + 4 * [(S.early1, 4)]
+    place, taken, seen = {}, [], []
+
+    def need(q, what):
+        if (q, what) not in seen:
+            seen.append((q, what))
+            q.wait_ge(*what)
+
+    def take(key, until):
+        if key not in place:
+            b = place[key] = (4 + len(taken)) % 8
+            taken.append(b)
+            need(P, freed[b])
+            freed[b] = until
+        return bank[place[key]]
+
+    def gather(q, o, lo, n):
+        q.wait_ge(S["w%d" % o], 1)
+        if o in folded:
+            move(q, T["ordq%d" % o][:, 16 * lo:16 * (lo + n)], win[o][:].indirect(T.placq[:, lo:lo + n]), S["g%d" % o])
         else:
-            product(o, bank[6][:, 0:256], 0, 256, S.my3a)
-            product(o, bank[7][:, 0:256], 256, 256, S.my3b)
-        if o < 2:
-            turn(o + 2)
+            move(q, T["ord%d" % o][:, 16 * lo:16 * (lo + n)], win[o][:].indirect(T.place[:, lo:lo + n]), S["g%d" % o])
 
-    def out_of(q, out, src, wait, n, sem):
-        q.wait_ge(wait, n)
-        if q is V:
-            V.tensor_copy(out, src).then_inc(sem, 1)
+    def order(q, o):
+        gather(q, o, 0, 32)
+
+    def half(q, o):
+        gather(q, o, 0 if q is V else 16, 16)
+
+    def fold(q, o):
+        need(V, gathered[o])
+        for t in range(4):
+            V.transpose(T["turned%d" % o][:, t:512:4], T["ordq%d" % o][:, 128 * t:128 * t + 128]).then_inc(S["vt%d" % o], 1)
+
+    def turn(o, t):
+        need(P, gathered[o])
+        if hready[o][1] == 1:
+            out, sem = take(("h", o), hready[o])[:, t:512:4], S["t%d0" % o]
         else:
-            A.activation(out, src, Copy).then_inc(sem, 1)
+            out, sem = take(("h", o, t), hready[o])[:, 0:128], S["t%d%d" % (o, t)]
+        P.transpose(out, T["ord%d" % o][:, t:512:4], T.ident[:]).then_inc(sem, 1)
 
-    def hcopy(q, o):
-        out_of(q, T.ht[:, 512 * o:512 * o + 512], bank[4 + o][:], S["t%d" % o], 4, S["hc%d" % o])
+    def product(o, k=None):
+        lo, n = (0, 512) if k is None else (256 * k, 256)
+        need(P, (S["qh%d" % o], 1))
+        P.matmul_mx(take(("y", o, k), yready[o])[:, 0:n], T.hc[:, 128 * o:128 * o + 128], T.hs[:, 128 * o:128 * o + 128],
+                    T.ac[:, lo:lo + n], T.ascale[:, lo:lo + n], True, True).then_inc(S["m%d%d" % (o, k or 0)], 1)
 
-    def hlast(q, t):
-        out_of(q, T.ht[:, 1536 + t:2048:4], bank[last[t]][:, 0:128], S["tl%d" % t], 1, S.hc3)
+    def hcopy(q, o, t=None):
+        if t is None:
+            out_of(q, T.ht[:, 512 * o:512 * o + 512], bank[place["h", o]][:], S["t%d0" % o], 4, S["h%d" % o])
+        else:
+            out_of(q, T.ht[:, 512 * o + t:512 * o + 512:4], bank[place["h", o, t]][:, 0:128], S["t%d%d" % (o, t)], 1, S["h%d" % o])
 
-    def hquant(o):
-        V.wait_ge(S["hc%d" % o], 1 if o < 3 else 4)
+    def quant(q, o):
+        need(V, hready[o])
         V.quantize_mx(T.hc[:, 128 * o:128 * o + 128], T.hs[:, 128 * o:128 * o + 128],
                       T.ht[:, 512 * o:512 * o + 512]).then_inc(S["qh%d" % o], 1)
 
-    def ycopy(q, o):
-        out_of(q, T.yt[:, 512 * o:512 * o + 512], bank[o][:], S["my%d" % o], 1, S["yc%d" % o])
+    def ycopy(q, o, k=None):
+        lo, n = (512 * o, 512) if k is None else (512 * o + 256 * k, 256)
+        out_of(q, T.yt[:, lo:lo + n], bank[place["y", o, k]][:, 0:n], S["m%d%d" % (o, k or 0)], 1, S["y%d" % o])
 
-    hquant(0)
-    hcopy(V, 1)
-    hquant(1)
-    ycopy(V, 1)
-    hquant(2)
-    hlast(V, 0)
-    hlast(V, 2)
-    hquant(3)
-    out_of(V, T.yt[:, 1536:1792], bank[6][:, 0:256], S.my3a, 1, S.yc3a)
+    def spread(q, o):
+        q.wait_ge(S["vt%d" % o], 4)
+        for k in range(4):
+            lo = 512 * o + 128 * k
+            q.dma_start(T.ht[:, lo:lo + 128], T["turned%d" % o][32 * k:32 * k + 32, :]).then_inc(S["h%d" % o], 16)
 
-    hcopy(A, 0)
-    ycopy(A, 0)
-    hcopy(A, 2)
-    hlast(A, 1)
-    hlast(A, 3)
-    ycopy(A, 2)
-    out_of(A, T.yt[:, 1792:2048], bank[7][:, 0:256], S.my3b, 1, S.yc3b)
-    A.wait_ge(S.yc3b, 1)
-    A.dma_start(T.y[:, 1792:2048], T.yt[:, 1792:2048]).then_inc(S.out, 16)
+    stores = []
 
-    for kind, o in (("h", 0), ("h", 1), ("y", 0), ("h", 2), ("y", 1), ("h", 3), ("y", 2)):
-        if kind == "h":
-            D.wait_ge(S["hc%d" % o], 1 if o < 3 else 4)
-            D.dma_start(T.h[:, 512 * o:512 * o + 512], T.ht[:, 512 * o:512 * o + 512]).then_inc(S.out, 16)
-        else:
-            D.wait_ge(S["yc%d" % o], 1)
-            D.dma_start(T.y[:, 512 * o:512 * o + 512], T.yt[:, 512 * o:512 * o + 512]).then_inc(S.out, 16)
-    D.wait_ge(S.yc3a, 1)
-    D.dma_start(T.y[:, 1536:1792], T.yt[:, 1536:1792]).then_inc(S.out, 16)
-    D.wait_ge(S.out, 16 * 9)
+    def hstore(q, o, n=1):
+        for k in range(o, o + n):
+            need(q, hready[k])
+        q.dma_start(T.h[:, 512 * o:512 * (o + n)], T.ht[:, 512 * o:512 * (o + n)]).then_inc(S.out, 16)
+        stores.append(o)
+
+    def ystore(q, o):
+        need(q, yready[o])
+        q.dma_start(T.y[:, 512 * o:512 * o + 512], T.yt[:, 512 * o:512 * o + 512]).then_inc(S.out, 16)
+        stores.append(o)
+
+    steps = {"unpack": unpack, "turn": turn, "product": product, "window": window, "order": order, "half": half, "fold": fold,
+             "hcopy": hcopy, "quant": quant, "ycopy": ycopy, "spread": spread, "hstore": hstore, "ystore": ystore}
+    for q, line in ((P, TENSOR), (V, VECTOR), (A, SCALAR), (D, SYNC)):
+        for name in line.split():
+            word = name.rstrip("0123")
+            numbers = [int(c) for c in name[len(word):]]
+            steps[word](*(numbers if q is P else [q] + numbers))
+    D.wait_ge(S.out, 16 * len(stores))
+    g.wait_ge(S.lsent, sum(listed))
     g.wait_ge(S.dsent, sum(sent))

@@ -7,12 +7,15 @@ PAD = 32
 WIN = 7 * CAPP
 ASKS = ((1, 2), (3, 4, 5, 6))
 SERVES = ((1, 2), (3, 4), (5, 6))
+EARLY = ((2,), (3, 2))
 
-TENSOR = ("unpack0 unpack3 unpack1 unpack2 turn00 turn01 turn02 turn03 turn10 turn11 turn12 turn13 product0 "
-          "turn20 turn21 turn22 turn23 product1 product20 product21 product3")
-VECTOR = "window0 half0 order3 fold3 hcopy0 quant0 hcopy1 hcopy20 quant1 hcopy22 hcopy23 quant2 quant3 ycopy21"
-SCALAR = "window3 half0 window1 order1 window2 order2 ycopy0 hcopy21 ycopy1 ycopy20 ycopy3"
-SYNC = "spread3 hstore0 hstore1 ystore0 hstore2 hstore3 ystore1 ystore2 ystore3"
+TENSOR = ("unpack0 unpack2 unpack1 unpack3 turn00 turn01 turn02 turn03 turn10 turn11 turn12 turn13 "
+          "product00 product01 product10 product11 product20 product21 product30 product31")
+VECTOR = ("window2 half0 half2 half1 fold2 half3 fold3 hcopy10 quant0 hcopy13 quant1 ycopy00 quant2 ycopy11 quant3 ycopy20 "
+          "ycopy30")
+SCALAR = ("window0 window1 half0 half2 window3 half1 half3 hcopy0 spread31 hcopy11 hcopy12 ycopy01 ycopy10 ycopy21 ycopy31 "
+          "ystore31")
+SYNC = "spread2 spread30 hstore0 hstore1 hstore2 ystore0 hstore3 ystore1 ystore2 ystore30"
 
 SCRATCH = {
     "wants": ("sbuf", [128, 42], "int32"),
@@ -29,7 +32,7 @@ SCRATCH = {
     "pickO": ("sbuf", [128, 512], "bfloat16"),
     "gotc": ("sbuf", [128, PAD + WIN], "float8_e4m3fn_x4"),
     "gots": ("sbuf", [128, PAD + WIN], "uint8"),
-    "num": ("sbuf", [128, 512], "bfloat16"),
+    "num": ("sbuf", [128, 256], "bfloat16"),
     "eye": ("sbuf", [128, 2048], "bfloat16"),
     "eyec": ("sbuf", [128, 512], "float8_e4m3fn_x4"),
     "eyes": ("sbuf", [128, 512], "uint8"),
@@ -56,7 +59,7 @@ for _b in range(8):
     SCRATCH["bank%d" % _b] = ("psum", [128, 512], "float32")
 
 SEMAPHORES = ["want", "vin", "slotin", "ain", "asks", "consts", "pad", "id", "eyeb", "eyeq", "lsent",
-              "list0", "list1", "gO", "qO", "p1", "p2", "p3", "q2", "q3", "qa", "dsent", "early0", "early1", "out"]
+              "list0", "list1", "gO", "qO", "p1", "p2", "p3", "q2", "q3", "qa", "dsent", "early0", "early1", "ylast", "out"]
 for _x in range(3):
     SEMAPHORES += ["gat%d" % _x, "qua%d" % _x, "data%d" % _x]
 for _o in range(4):
@@ -73,10 +76,14 @@ def fused(g, core, topo, parts, remote_sem, local_sem):
     for i, (d, src, dst) in enumerate(parts):
         rid, pid, _ = topo.addr(d)
         transfers.append(RemoteDMATransfer(dst_ids=[DstId(rid=rid, pnc=pid)],
-                                           dma_engine_mask=sum(1 << e for e in engines[i * w:(i + 1) * w]),
+                                           dma_engine_mask=sum(1 << e for e in engines[i::len(parts)][:w]),
                                            remote_sem=remote_sem, src=src, dst=dst))
     g.remote_dma_fused(transfers, local_sem=local_sem)
     return w
+
+
+def hops(topo, a, b):
+    return 1 if topo.mates(topo.chip(a), topo.chip(b)) or topo.same_plane(topo.chip(a), topo.chip(b)) else 2
 
 
 def rank_program(g, core, T, topo):
@@ -100,9 +107,8 @@ def rank_program(g, core, T, topo):
         q.wait_ge(wait, n)
         move(q, out, src, sem)
 
-    for k in range(4):
-        D.dma_start(T.wants[16 * k:16 * k + 16, :], T.want[:]).then_inc(S.want, 16)
-        A.dma_start(T.wants[64 + 16 * k:64 + 16 * k + 16, :], T.want[:]).then_inc(S.want, 16)
+    D.dma_start(T.wants[0:16, :], T.want[:]).then_inc(S.want, 16)
+    A.dma_start(T.wants[16:32, :], T.want[:]).then_inc(S.want, 16)
     D.dma_start(T.vt[:], T.v[:]).then_inc(S.vin, 16)
     for k in range(2):
         D.dma_start(T.slots[16 * k:16 * k + 16, 0:32], T.slot[:]).then_inc(S.slotin, 16)
@@ -110,8 +116,8 @@ def rank_program(g, core, T, topo):
         D.dma_start(T.slots[8 * t:8 * t + 8, 32:48], T.slot[t:16:4, :]).then_inc(S.slotin, 16)
     D.dma_start(T.at[:], T.a[:]).then_inc(S.ain, 16)
 
-    g.iota(T.num[:], [[1, 512]], 0, -4, allow_small_or_imprecise_dtypes=True).then_inc(S.consts, 1)
-    g.wait_ge(S.asks, 1)
+    g.iota(T.num[:], [[1, 256]], 128, -4, allow_small_or_imprecise_dtypes=True).then_inc(S.consts, 1)
+    g.wait_ge(S.asks, 4)
     listed = []
     for x, ds in enumerate(ASKS):
         parts = []
@@ -121,33 +127,44 @@ def rank_program(g, core, T, topo):
         listed.append(len(parts) * fused(g, core, topo, parts, S["list%d" % x], S.lsent))
 
     V.memset(T.pickO[:, 0:4 * PAD], 0.0).then_inc(S.pad, 1)
-    V.wait_ge(S.want, 128)
-    V.tensor_scalar(T.ask[:], T.wants[:], 4.0, 0.0, AluOpType.mult, AluOpType.max).then_inc(S.asks, 1)
+    V.wait_ge(S.want, 32)
+    for lo in (0, 32, 64, 96):
+        V.tensor_scalar(T.ask[lo:lo + 32, :], T.wants[0:32, :], 4.0, 0.0, AluOpType.mult, AluOpType.max).then_inc(S.asks, 1)
     V.wait_ge(S.consts, 1)
-    for t in range(4):
-        V.tensor_scalar(T.eye[:, t:2048:4], T.num[:], float(t), None, AluOpType.is_equal).then_inc(S.eyeb, 1)
-    V.tensor_scalar(T.ident[:], T.num[:, 0:512:4], 0.0, None, AluOpType.is_equal).then_inc(S.id, 1)
-    V.wait_ge(S.eyeb, 4)
+    for k in range(2):
+        for t in range(4):
+            V.tensor_scalar(T.eye[:, 1024 * k + t:1024 * k + 1024:4], T.num[:], float(128 - 256 * k + t), None,
+                            AluOpType.is_equal).then_inc(S.eyeb, 1)
+        V.tensor_scalar(T.ident[:, 64 * k:64 * k + 64], T.num[:, 0:256:4], float(128 - 256 * k), None,
+                        AluOpType.is_equal).then_inc(S.id, 1)
+    V.wait_ge(S.eyeb, 8)
     V.quantize_mx(T.eyec[:], T.eyes[:], T.eye[:]).then_inc(S.eyeq, 1)
 
     def pick(tile, lo, offsets, sem, who):
-        n4 = tile.shape[1]
+        hi = lo + 64 * offsets.shape[1]
         for t in range(4):
-            move(who[t], tile[:, lo + t:n4:4], T.vt[:, t:2048].indirect(offsets), sem)
+            move(who[t], tile[:, lo + t:hi:4], T.vt[:, t:2048].indirect(offsets), sem)
 
     V.wait_ge(S.vin, 16)
     A.wait_ge(S.vin, 16)
-    A.wait_ge(S.asks, 1)
+    A.wait_ge(S.asks, 4)
     pick(T.pickO, 4 * PAD, T.ask[:, KO * rank:KO * rank + KO], S.gO, (A, A, A, A))
-    sent = [0, 0, 0]
+    V.wait_ge(S.gO, 4)
+    V.wait_ge(S.pad, 1)
+    V.quantize_mx(T.gotc[:, 0:PAD + CAPP], T.gots[:, 0:PAD + CAPP], T.pickO[:]).then_inc(S.qO, 1)
+    sent, lanes = [0] * len(SERVES), [0, 0]
     for x, ds in enumerate(SERVES):
         if x < len(ASKS):
             V.wait_ge(S["list%d" % x], listed[x])
             A.wait_ge(S["list%d" % x], listed[x])
         gs, qs = S["gat%d" % x], S["qua%d" % x]
         code, scal, tile = T["code%d" % x], T["scal%d" % x], T["pick%d" % x]
-        pick(tile, 0, T.asked[:, KO * (ds[0] - 1):KO * ds[-1]], gs, (V, V, A, A))
-        V.wait_ge(gs, 4)
+        lo, hi = KO * (ds[0] - 1), KO * ds[1]
+        mid = hi - KO if x == 2 else hi
+        calls = [c for c in ((V, 0, lo, hi), (V, 1, lo, mid), (A, 1, mid, hi), (A, 2, lo, hi), (A, 3, lo, hi)) if c[2] < c[3]]
+        for q, t, a, b in calls:
+            move(q, tile[:, 64 * (a - lo) + t:64 * (b - lo):4], T.vt[:, t:2048].indirect(T.asked[:, a:b]), gs)
+        V.wait_ge(gs, len(calls))
         V.quantize_mx(code[:], scal[:], tile[:]).then_inc(qs, 1)
         g.wait_ge(qs, 1)
         cparts, sparts = [], []
@@ -156,12 +173,13 @@ def rank_program(g, core, T, topo):
             to = PAD + CAPP * d
             cparts.append((dst, code[:, CAPP * i:CAPP * i + CAPP].bitcast(dt.uint8), T.gotc[:, to:to + CAPP].bitcast(dt.uint8)))
             sparts.append((dst, scal[:, CAPP * i:CAPP * i + CAPP], T.gots[:, to:to + CAPP]))
+        far = [hops(topo, core, dst) for dst, _, _ in cparts]
+        if (far[0] - far[1]) * (lanes[0] - lanes[1]) > 0:
+            cparts, sparts, far = cparts[::-1], sparts[::-1], far[::-1]
+        lanes = [lanes[0] + far[0], lanes[1] + far[1]]
         for parts in (cparts, sparts):
             sent[x] += len(parts) * fused(g, core, topo, parts, S["data%d" % x], S.dsent)
 
-    V.wait_ge(S.gO, 4)
-    V.wait_ge(S.pad, 1)
-    V.quantize_mx(T.gotc[:, 0:PAD + CAPP], T.gots[:, 0:PAD + CAPP], T.pickO[:]).then_inc(S.qO, 1)
     first, add, sub = float(CAPP * rank), AluOpType.add, AluOpType.subtract
     V.wait_ge(S.slotin, 96)
     V.tensor_scalar(T.wraps[0:32, :], T.slots[0:32, :], first, float(WIN), AluOpType.is_lt, AluOpType.mult).then_inc(S.p1, 1)
@@ -180,38 +198,39 @@ def rank_program(g, core, T, topo):
     V.wait_ge(S.q3, 1)
     V.tensor_scalar(T.placq[:], T.movt[:], first, None, sub).then_inc(S.p3, 1)
 
-    spans = ((0, 3 * CAPP, 0), (3 * CAPP, 2 * CAPP, 4), (5 * CAPP, 2 * CAPP, 0))
+    spans = ((0, 3 * CAPP, 0), (3 * CAPP, 5 * CAPP, 4), (5 * CAPP, 7 * CAPP, 0))
 
     def unpack(o, x=2):
-        lo, n, b = spans[x]
-        P.matmul_mx(bank[b + o][:, 0:n], T.eyec[:, 128 * o:128 * o + 128], T.eyes[:, 128 * o:128 * o + 128],
-                    T.gotc[:, PAD + lo:PAD + lo + n], T.gots[:, PAD + lo:PAD + lo + n], True, True).then_inc(S["u%d%d" % (x, o)], 1)
+        lo, hi, b = spans[x]
+        P.matmul_mx(bank[b + o][:, 0:hi - lo], T.eyec[:, 128 * o:128 * o + 128], T.eyes[:, 128 * o:128 * o + 128],
+                    T.gotc[:, PAD + lo:PAD + hi], T.gots[:, PAD + lo:PAD + hi], True, True).then_inc(S["u%d%d" % (x, o)], 1)
 
     def window(q, o, x=2):
-        lo, n, b = spans[x]
-        out_of(q, win[o][:, lo:lo + n], bank[b + o][:, 0:n], S["u%d%d" % (x, o)], 1, S["w%d" % o if x == 2 else "early%d" % x])
+        lo, hi, b = spans[x]
+        out_of(q, win[o][:, lo:hi], bank[b + o][:, 0:hi - lo], S["u%d%d" % (x, o)], 1, S["w%d" % o if x == 2 else "early%d" % x])
 
     P.wait_ge(S.eyeq, 1)
-    P.wait_ge(S.id, 1)
+    P.wait_ge(S.id, 2)
     P.wait_ge(S.qO, 1)
     for x in (0, 1):
         P.wait_ge(S["data%d" % x], sent[x])
         for o in (0, 3, 1, 2):
             unpack(o, x)
-            window(A if o < 2 else V, o, x)
-        for q in (V, A):
-            if x == 0:
-                q.wait_ge(S.p3, 2)
-            q.wait_ge(S["early%d" % x], 4)
+            window(V if o in EARLY[x] else A, o, x)
+    V.wait_ge(S.p3, 2)
+    A.wait_ge(S.p3, 2)
+    for q in (V, A, P):
+        q.wait_ge(S.early0, 4)
     P.wait_ge(S.qa, 1)
-    P.wait_ge(S.early0, 4)
     P.wait_ge(S.data2, sent[2])
+
 
     names = (TENSOR + " " + VECTOR + " " + SCALAR).split()
     folded = [o for o in range(4) if "fold%d" % o in names]
     gathered = [(S["g%d" % o], 2 if "half%d" % o in names else 1) for o in range(4)]
     hready = [(S["h%d" % o], 64 if o in folded else 1 if "hcopy%d" % o in names else 4) for o in range(4)]
-    yready = [(S["y%d" % o], 1 if "ycopy%d" % o in names else 2) for o in range(4)]
+    apart = [o for o in range(4) if "ystore%d0" % o in names + SYNC.split()]
+    yready = [(S["y%d" % o], 1 if "ycopy%d" % o in names or o in apart else 2) for o in range(4)]
     freed = [(S["w%d" % b], 1) for b in range(4)] + 4 * [(S.early1, 4)]
     place, taken, seen = {}, [], []
 
@@ -229,6 +248,7 @@ def rank_program(g, core, T, topo):
         return bank[place[key]]
 
     def gather(q, o, lo, n):
+        need(q, (S.early1, 4))
         q.wait_ge(S["w%d" % o], 1)
         if o in folded:
             move(q, T["ordq%d" % o][:, 16 * lo:16 * (lo + n)], win[o][:].indirect(T.placq[:, lo:lo + n]), S["g%d" % o])
@@ -273,11 +293,12 @@ def rank_program(g, core, T, topo):
 
     def ycopy(q, o, k=None):
         lo, n = (512 * o, 512) if k is None else (512 * o + 256 * k, 256)
-        out_of(q, T.yt[:, lo:lo + n], bank[place["y", o, k]][:, 0:n], S["m%d%d" % (o, k or 0)], 1, S["y%d" % o])
+        out_of(q, T.yt[:, lo:lo + n], bank[place["y", o, k]][:, 0:n], S["m%d%d" % (o, k or 0)], 1,
+               S.ylast if o in apart and k else S["y%d" % o])
 
-    def spread(q, o):
-        q.wait_ge(S["vt%d" % o], 4)
-        for k in range(4):
+    def spread(q, o, j=None):
+        need(q, (S["vt%d" % o], 4))
+        for k in range(4) if j is None else (2 * j, 2 * j + 1):
             lo = 512 * o + 128 * k
             q.dma_start(T.ht[:, lo:lo + 128], T["turned%d" % o][32 * k:32 * k + 32, :]).then_inc(S["h%d" % o], 16)
 
@@ -289,9 +310,10 @@ def rank_program(g, core, T, topo):
         q.dma_start(T.h[:, 512 * o:512 * (o + n)], T.ht[:, 512 * o:512 * (o + n)]).then_inc(S.out, 16)
         stores.append(o)
 
-    def ystore(q, o):
-        need(q, yready[o])
-        q.dma_start(T.y[:, 512 * o:512 * o + 512], T.yt[:, 512 * o:512 * o + 512]).then_inc(S.out, 16)
+    def ystore(q, o, k=None):
+        lo, n = (512 * o, 512) if k is None else (512 * o + 256 * k, 256)
+        need(q, (S.ylast, 1) if k else yready[o])
+        q.dma_start(T.y[:, lo:lo + n], T.yt[:, lo:lo + n]).then_inc(S.out, 16)
         stores.append(o)
 
     steps = {"unpack": unpack, "turn": turn, "product": product, "window": window, "order": order, "half": half, "fold": fold,

from concourse.bass import DstId, RemoteDMATransfer
from concourse.mybir import dt, AluOpType, ActivationFunctionType

CAPP = 96
KO = CAPP // 16
PAD = 32
WIN = 7 * CAPP
ASKS = ((1, 2), (3, 4, 5, 6))
SERVES = ((1, 2), (3, 4), (5, 6))
EARLY = ((2,), (3, 2))

TENSOR = ("unpack0 unpack2 unpack1 unpack3 turn00 turn01 turn02 turn03 turn10 turn11 turn12 turn13 "
          "product00 product01 product10 product11 product20 product21 product30 product31")
VECTOR = ("window2 half0 half2 half1 fold2 half3 fold3 hcopy10 quant0 hcopy13 quant1 ycopy00 quant2 ycopy11 quant3 ycopy20 "
          "ycopy30")
SCALAR = ("window0 window1 half0 half2 window3 half1 half3 hcopy0 spread31 hcopy11 hcopy12 ycopy01 ycopy10 ycopy21 ycopy31 "
          "ystore31")
SYNC = "spread2 spread30 hstore0 hstore1 hstore2 ystore0 hstore3 ystore1 ystore2 ystore30"

SCRATCH = {
    "wants": ("sbuf", [128, 42], "int32"),
    "slots": ("sbuf", [128, 48], "int32"),
    "wraps": ("sbuf", [128, 48], "int32"),
    "moved": ("sbuf", [128, 64], "float32"),
    "movt": ("sbuf", [128, 32], "float32"),
    "ask": ("sbuf", [128, 42], "uint16"),
    "asked": ("sbuf", [128, 36], "uint16"),
    "place": ("sbuf", [128, 32], "uint16"),
    "placq": ("sbuf", [128, 32], "uint16"),
    "vt": ("sbuf", [128, 2048], "bfloat16"),
    "at": ("sbuf", [128, 2048], "bfloat16"),
    "pickO": ("sbuf", [128, 512], "bfloat16"),
    "gotc": ("sbuf", [128, PAD + WIN], "float8_e4m3fn_x4"),
    "gots": ("sbuf", [128, PAD + WIN], "uint8"),
    "num": ("sbuf", [128, 256], "bfloat16"),
    "eye": ("sbuf", [128, 2048], "bfloat16"),
    "eyec": ("sbuf", [128, 512], "float8_e4m3fn_x4"),
    "eyes": ("sbuf", [128, 512], "uint8"),
    "ident": ("sbuf", [128, 128], "float32"),
    "ht": ("sbuf", [128, 2048], "bfloat16"),
    "hc": ("sbuf", [128, 512], "float8_e4m3fn_x4"),
    "hs": ("sbuf", [128, 512], "uint8"),
    "ac": ("sbuf", [128, 512], "float8_e4m3fn_x4"),
    "ascale": ("sbuf", [128, 512], "uint8"),
    "yt": ("sbuf", [128, 2048], "float32"),
}
for _x in range(3):
    SCRATCH["pick%d" % _x] = ("sbuf", [128, 8 * CAPP], "bfloat16")
    SCRATCH["code%d" % _x] = ("sbuf", [128, 2 * CAPP], "float8_e4m3fn_x4")
    SCRATCH["scal%d" % _x] = ("sbuf", [128, 2 * CAPP], "uint8")
for _o in range(4):
    SCRATCH["win%d" % _o] = ("sbuf", [128, WIN], "bfloat16")
    if "fold%d" % _o in VECTOR:
        SCRATCH["ordq%d" % _o] = ("sbuf", [128, 512], "bfloat16")
        SCRATCH["turned%d" % _o] = ("sbuf", [128, 512], "bfloat16")
    else:
        SCRATCH["ord%d" % _o] = ("sbuf", [128, 512], "float32")
for _b in range(8):
    SCRATCH["bank%d" % _b] = ("psum", [128, 512], "float32")

SEMAPHORES = ["want", "vin", "slotin", "ain", "asks", "consts", "pad", "id", "eyeb", "eyeq", "lsent",
              "list0", "list1", "gO", "qO", "p1", "p2", "p3", "q2", "q3", "qa", "dsent", "early0", "early1", "ylast", "out"]
for _x in range(3):
    SEMAPHORES += ["gat%d" % _x, "qua%d" % _x, "data%d" % _x]
for _o in range(4):
    SEMAPHORES += [_c + "%d" % _o for _c in ("w", "g", "vt", "h", "qh", "y")]
    SEMAPHORES += ["u%d%d" % (_x, _o) for _x in range(3)] + ["t%d%d" % (_o, _x) for _x in range(4)] + ["m%d0" % _o, "m%d1" % _o]


def fused(g, core, topo, parts, remote_sem, local_sem):
    engines = [e for e in topo.engines(core, parts[0][0]) if all(e in topo.engines(core, d) for d, _, _ in parts)]
    w = 1
    while 2 * w * len(parts) <= len(engines):
        w *= 2
    transfers = []
    for i, (d, src, dst) in enumerate(parts):
        rid, pid, _ = topo.addr(d)
        transfers.append(RemoteDMATransfer(dst_ids=[DstId(rid=rid, pnc=pid)],
                                           dma_engine_mask=sum(1 << e for e in engines[i::len(parts)][:w]),
                                           remote_sem=remote_sem, src=src, dst=dst))
    g.remote_dma_fused(transfers, local_sem=local_sem)
    return w


def hops(topo, a, b):
    return 1 if topo.mates(topo.chip(a), topo.chip(b)) or topo.same_plane(topo.chip(a), topo.chip(b)) else 2


def rank_program(g, core, T, topo):
    rank = T.rank_of(core)
    if rank is None:
        return
    N = len(T.cores)
    S = T.sem
    V, A, P, D = g.vector, g.scalar, g.tensor, g.sync
    Copy = ActivationFunctionType.Copy
    bank = [T["bank%d" % b] for b in range(8)]
    win = [T["win%d" % o] for o in range(4)]

    def move(q, out, src, sem):
        if q is V:
            V.tensor_copy(out, src).then_inc(sem, 1)
        else:
            A.activation(out, src, Copy).then_inc(sem, 1)

    def out_of(q, out, src, wait, n, sem):
        q.wait_ge(wait, n)
        move(q, out, src, sem)

    D.dma_start(T.wants[0:16, :], T.want[:]).then_inc(S.want, 16)
    A.dma_start(T.wants[16:32, :], T.want[:]).then_inc(S.want, 16)
    D.dma_start(T.vt[:], T.v[:]).then_inc(S.vin, 16)
    for k in range(2):
        D.dma_start(T.slots[16 * k:16 * k + 16, 0:32], T.slot[:]).then_inc(S.slotin, 16)
    for t in range(4):
        D.dma_start(T.slots[8 * t:8 * t + 8, 32:48], T.slot[t:16:4, :]).then_inc(S.slotin, 16)
    D.dma_start(T.at[:], T.a[:]).then_inc(S.ain, 16)

    g.iota(T.num[:], [[1, 256]], 128, -4, allow_small_or_imprecise_dtypes=True).then_inc(S.consts, 1)
    g.wait_ge(S.asks, 4)
    listed = []
    for x, ds in enumerate(ASKS):
        parts = []
        for d in ds:
            q = (rank + d) % N
            parts.append((T.cores[q], T.ask[:, KO * q:KO * q + KO], T.asked[:, KO * (d - 1):KO * d]))
        listed.append(len(parts) * fused(g, core, topo, parts, S["list%d" % x], S.lsent))

    V.memset(T.pickO[:, 0:4 * PAD], 0.0).then_inc(S.pad, 1)
    V.wait_ge(S.want, 32)
    for lo in (0, 32, 64, 96):
        V.tensor_scalar(T.ask[lo:lo + 32, :], T.wants[0:32, :], 4.0, 0.0, AluOpType.mult, AluOpType.max).then_inc(S.asks, 1)
    V.wait_ge(S.consts, 1)
    for k in range(2):
        for t in range(4):
            V.tensor_scalar(T.eye[:, 1024 * k + t:1024 * k + 1024:4], T.num[:], float(128 - 256 * k + t), None,
                            AluOpType.is_equal).then_inc(S.eyeb, 1)
        V.tensor_scalar(T.ident[:, 64 * k:64 * k + 64], T.num[:, 0:256:4], float(128 - 256 * k), None,
                        AluOpType.is_equal).then_inc(S.id, 1)
    V.wait_ge(S.eyeb, 8)
    V.quantize_mx(T.eyec[:], T.eyes[:], T.eye[:]).then_inc(S.eyeq, 1)

    def pick(tile, lo, offsets, sem, who):
        hi = lo + 64 * offsets.shape[1]
        for t in range(4):
            move(who[t], tile[:, lo + t:hi:4], T.vt[:, t:2048].indirect(offsets), sem)

    V.wait_ge(S.vin, 16)
    A.wait_ge(S.vin, 16)
    A.wait_ge(S.asks, 4)
    pick(T.pickO, 4 * PAD, T.ask[:, KO * rank:KO * rank + KO], S.gO, (A, A, A, A))
    V.wait_ge(S.gO, 4)
    V.wait_ge(S.pad, 1)
    V.quantize_mx(T.gotc[:, 0:PAD + CAPP], T.gots[:, 0:PAD + CAPP], T.pickO[:]).then_inc(S.qO, 1)
    sent, lanes = [0] * len(SERVES), [0, 0]
    for x, ds in enumerate(SERVES):
        if x < len(ASKS):
            V.wait_ge(S["list%d" % x], listed[x])
            A.wait_ge(S["list%d" % x], listed[x])
        gs, qs = S["gat%d" % x], S["qua%d" % x]
        code, scal, tile = T["code%d" % x], T["scal%d" % x], T["pick%d" % x]
        lo, hi = KO * (ds[0] - 1), KO * ds[1]
        mid = hi - KO if x == 2 else hi
        calls = [c for c in ((V, 0, lo, hi), (V, 1, lo, mid), (A, 1, mid, hi), (A, 2, lo, hi), (A, 3, lo, hi)) if c[2] < c[3]]
        for q, t, a, b in calls:
            move(q, tile[:, 64 * (a - lo) + t:64 * (b - lo):4], T.vt[:, t:2048].indirect(T.asked[:, a:b]), gs)
        V.wait_ge(gs, len(calls))
        V.quantize_mx(code[:], scal[:], tile[:]).then_inc(qs, 1)
        g.wait_ge(qs, 1)
        cparts, sparts = [], []
        for i, d in enumerate(ds):
            dst = T.cores[(rank - d) % N]
            to = PAD + CAPP * d
            cparts.append((dst, code[:, CAPP * i:CAPP * i + CAPP].bitcast(dt.uint8), T.gotc[:, to:to + CAPP].bitcast(dt.uint8)))
            sparts.append((dst, scal[:, CAPP * i:CAPP * i + CAPP], T.gots[:, to:to + CAPP]))
        far = [hops(topo, core, dst) for dst, _, _ in cparts]
        if (far[0] - far[1]) * (lanes[0] - lanes[1]) > 0:
            cparts, sparts, far = cparts[::-1], sparts[::-1], far[::-1]
        lanes = [lanes[0] + far[0], lanes[1] + far[1]]
        for parts in (cparts, sparts):
            sent[x] += len(parts) * fused(g, core, topo, parts, S["data%d" % x], S.dsent)

    first, add, sub = float(CAPP * rank), AluOpType.add, AluOpType.subtract
    V.wait_ge(S.slotin, 96)
    V.tensor_scalar(T.wraps[0:32, :], T.slots[0:32, :], first, float(WIN), AluOpType.is_lt, AluOpType.mult).then_inc(S.p1, 1)
    V.wait_ge(S.p1, 1)
    V.tensor_tensor(T.moved[0:32, 0:48], T.slots[0:32, :], T.wraps[0:32, :], add).then_inc(S.q2, 1)
    V.tensor_tensor(T.moved[0:32, 48:64], T.slots[0:32, 32:48], T.wraps[0:32, 32:48], add).then_inc(S.q2, 1)
    A.wait_ge(S.q2, 2)
    for k in range(1, 4):
        move(A, T.moved[32 * k:32 * k + 32, :], T.moved[0:32, :], S.p2)
    V.wait_ge(S.ain, 16)
    V.quantize_mx(T.ac[:], T.ascale[:], T.at[:]).then_inc(S.qa, 1)
    V.wait_ge(S.q2, 2)
    V.wait_ge(S.p2, 3)
    V.transpose(T.movt[:], T.moved[:, 32:64]).then_inc(S.q3, 1)
    V.tensor_scalar(T.place[:], T.moved[:, 0:32], first, None, sub).then_inc(S.p3, 1)
    V.wait_ge(S.q3, 1)
    V.tensor_scalar(T.placq[:], T.movt[:], first, None, sub).then_inc(S.p3, 1)

    spans = ((0, 3 * CAPP, 0), (3 * CAPP, 5 * CAPP, 4), (5 * CAPP, 7 * CAPP, 0))

    def unpack(o, x=2):
        lo, hi, b = spans[x]
        P.matmul_mx(bank[b + o][:, 0:hi - lo], T.eyec[:, 128 * o:128 * o + 128], T.eyes[:, 128 * o:128 * o + 128],
                    T.gotc[:, PAD + lo:PAD + hi], T.gots[:, PAD + lo:PAD + hi], True, True).then_inc(S["u%d%d" % (x, o)], 1)

    def window(q, o, x=2):
        lo, hi, b = spans[x]
        out_of(q, win[o][:, lo:hi], bank[b + o][:, 0:hi - lo], S["u%d%d" % (x, o)], 1, S["w%d" % o if x == 2 else "early%d" % x])

    P.wait_ge(S.eyeq, 1)
    P.wait_ge(S.id, 2)
    P.wait_ge(S.qO, 1)
    for x in (0, 1):
        P.wait_ge(S["data%d" % x], sent[x])
        for o in (0, 3, 1, 2):
            unpack(o, x)
            window(V if o in EARLY[x] else A, o, x)
    V.wait_ge(S.p3, 2)
    A.wait_ge(S.p3, 2)
    for q in (V, A, P):
        q.wait_ge(S.early0, 4)
    P.wait_ge(S.qa, 1)
    P.wait_ge(S.data2, sent[2])


    names = (TENSOR + " " + VECTOR + " " + SCALAR).split()
    folded = [o for o in range(4) if "fold%d" % o in names]
    gathered = [(S["g%d" % o], 2 if "half%d" % o in names else 1) for o in range(4)]
    hready = [(S["h%d" % o], 64 if o in folded else 1 if "hcopy%d" % o in names else 4) for o in range(4)]
    apart = [o for o in range(4) if "ystore%d0" % o in names + SYNC.split()]
    yready = [(S["y%d" % o], 1 if "ycopy%d" % o in names or o in apart else 2) for o in range(4)]
    freed = [(S["w%d" % b], 1) for b in range(4)] + 4 * [(S.early1, 4)]
    place, taken, seen = {}, [], []

    def need(q, what):
        if (q, what) not in seen:
            seen.append((q, what))
            q.wait_ge(*what)

    def take(key, until):
        if key not in place:
            b = place[key] = (4 + len(taken)) % 8
            taken.append(b)
            need(P, freed[b])
            freed[b] = until
        return bank[place[key]]

    def gather(q, o, lo, n):
        need(q, (S.early1, 4))
        q.wait_ge(S["w%d" % o], 1)
        if o in folded:
            move(q, T["ordq%d" % o][:, 16 * lo:16 * (lo + n)], win[o][:].indirect(T.placq[:, lo:lo + n]), S["g%d" % o])
        else:
            move(q, T["ord%d" % o][:, 16 * lo:16 * (lo + n)], win[o][:].indirect(T.place[:, lo:lo + n]), S["g%d" % o])

    def order(q, o):
        gather(q, o, 0, 32)

    def half(q, o):
        gather(q, o, 0 if q is V else 16, 16)

    def fold(q, o):
        need(V, gathered[o])
        for t in range(4):
            V.transpose(T["turned%d" % o][:, t:512:4], T["ordq%d" % o][:, 128 * t:128 * t + 128]).then_inc(S["vt%d" % o], 1)

    def turn(o, t):
        need(P, gathered[o])
        if hready[o][1] == 1:
            out, sem = take(("h", o), hready[o])[:, t:512:4], S["t%d0" % o]
        else:
            out, sem = take(("h", o, t), hready[o])[:, 0:128], S["t%d%d" % (o, t)]
        P.transpose(out, T["ord%d" % o][:, t:512:4], T.ident[:]).then_inc(sem, 1)

    def product(o, k=None):
        lo, n = (0, 512) if k is None else (256 * k, 256)
        need(P, (S["qh%d" % o], 1))
        P.matmul_mx(take(("y", o, k), yready[o])[:, 0:n], T.hc[:, 128 * o:128 * o + 128], T.hs[:, 128 * o:128 * o + 128],
                    T.ac[:, lo:lo + n], T.ascale[:, lo:lo + n], True, True).then_inc(S["m%d%d" % (o, k or 0)], 1)

    def hcopy(q, o, t=None):
        if t is None:
            out_of(q, T.ht[:, 512 * o:512 * o + 512], bank[place["h", o]][:], S["t%d0" % o], 4, S["h%d" % o])
        else:
            out_of(q, T.ht[:, 512 * o + t:512 * o + 512:4], bank[place["h", o, t]][:, 0:128], S["t%d%d" % (o, t)], 1, S["h%d" % o])

    def quant(q, o):
        need(V, hready[o])
        V.quantize_mx(T.hc[:, 128 * o:128 * o + 128], T.hs[:, 128 * o:128 * o + 128],
                      T.ht[:, 512 * o:512 * o + 512]).then_inc(S["qh%d" % o], 1)

    def ycopy(q, o, k=None):
        lo, n = (512 * o, 512) if k is None else (512 * o + 256 * k, 256)
        out_of(q, T.yt[:, lo:lo + n], bank[place["y", o, k]][:, 0:n], S["m%d%d" % (o, k or 0)], 1,
               S.ylast if o in apart and k else S["y%d" % o])

    def spread(q, o, j=None):
        need(q, (S["vt%d" % o], 4))
        for k in range(4) if j is None else (2 * j, 2 * j + 1):
            lo = 512 * o + 128 * k
            q.dma_start(T.ht[:, lo:lo + 128], T["turned%d" % o][32 * k:32 * k + 32, :]).then_inc(S["h%d" % o], 16)

    stores = []

    def hstore(q, o, n=1):
        for k in range(o, o + n):
            need(q, hready[k])
        q.dma_start(T.h[:, 512 * o:512 * (o + n)], T.ht[:, 512 * o:512 * (o + n)]).then_inc(S.out, 16)
        stores.append(o)

    def ystore(q, o, k=None):
        lo, n = (512 * o, 512) if k is None else (512 * o + 256 * k, 256)
        need(q, (S.ylast, 1) if k else yready[o])
        q.dma_start(T.y[:, lo:lo + n], T.yt[:, lo:lo + n]).then_inc(S.out, 16)
        stores.append(o)

    steps = {"unpack": unpack, "turn": turn, "product": product, "window": window, "order": order, "half": half, "fold": fold,
             "hcopy": hcopy, "quant": quant, "ycopy": ycopy, "spread": spread, "hstore": hstore, "ystore": ystore}
    for q, line in ((P, TENSOR), (V, VECTOR), (A, SCALAR), (D, SYNC)):
        for name in line.split():
            word = name.rstrip("0123")
            numbers = [int(c) for c in name[len(word):]]
            steps[word](*(numbers if q is P else [q] + numbers))
    D.wait_ge(S.out, 16 * len(stores))
    g.wait_ge(S.lsent, sum(listed))
    g.wait_ge(S.dsent, sum(sent))
